import numpy as np
import ml_dtypes


def mxq(x, axis, fmt="e4m3"):
    dtype, down = {"e4m3": (ml_dtypes.float8_e4m3fn, 7), "e5m2": (ml_dtypes.float8_e5m2, 14)}[fmt]
    v = np.moveaxis(np.asarray(x, np.float32).astype(ml_dtypes.bfloat16).astype(np.float64), axis, -1)
    blocks = v.reshape(v.shape[:-1] + (-1, 32))
    amax = np.abs(blocks).max(-1, keepdims=True)
    byte = np.maximum(np.where(amax > 0, np.frexp(amax)[1] - 1 + 127, 0) - down, 1)
    scale = np.exp2(byte - 127.0)
    codes = (blocks / scale).astype(np.float32).astype(dtype).astype(np.float64)
    return np.moveaxis((codes * scale).reshape(v.shape), -1, axis)


WIDE = False


def mx_kscale(k):
    if not WIDE:
        return np.ones(k)
    levels = np.array([10, -10, 5, -5, 0])
    if k % 512:
        return np.exp2(np.random.permutation(np.resize(levels, k // 32))).repeat(32)
    a = np.empty((k // 512, 16))
    for p in range(k // 512):
        a[p, :8] = np.random.permutation(np.resize(levels, 8))
        for g in range(8):
            far = levels[np.abs(levels - a[p, g]) >= 10]
            a[p, g + 8] = far[np.random.randint(len(far))]
    return np.exp2(a.ravel()).repeat(32)


def f64(x):
    return np.asarray(x).astype(np.float64)


def striped(idx):
    return np.tile(idx.reshape(-1, 16).T, (8, 1)).astype(np.uint16)


def unstriped(offs):
    return offs[:16].T.reshape(-1).astype(np.int64)


E2M1 = np.array([0.0, 0.5, 1.0, 1.5, 2.0, 3.0, 4.0, 6.0, -0.0, -0.5, -1.0, -1.5, -2.0, -3.0, -4.0, -6.0])


def pack_weight(w, fmt):
    k, n = w.shape
    w = f64(np.asarray(w, np.float32).astype(ml_dtypes.bfloat16)).reshape(k // 32, 32, n)
    amax = np.abs(w).max(1)
    if fmt == "e4m3":
        byte = np.frexp(amax)[1] - 1 + 127 - 7
    else:
        mant, ex = np.frexp(amax / 6.0)
        byte = np.where(mant > 0.5, ex, ex - 1) + 127
    byte = np.clip(np.where(amax > 0, byte, 1), 1, 254)
    scaled = (w * np.exp2(127.0 - byte)[:, None, :]).reshape(k, n).astype(np.float32)
    by_word = np.ascontiguousarray(scaled.reshape(k // 512, 128, 4, n).transpose(0, 1, 3, 2))
    if fmt == "e4m3":
        words = by_word.astype(ml_dtypes.float8_e4m3fn).view(np.uint8)
    else:
        c = by_word.astype(ml_dtypes.float4_e2m1fn).view(np.uint8) & 0xF
        words = (c[..., 0::2] | (c[..., 1::2] << 4)).reshape(k // 512, 128, 2 * n)
    return np.ascontiguousarray(words), np.ascontiguousarray(byte.astype(np.uint8).reshape(k // 512, 16, n))


def unpack_weight(words, scales, fmt):
    g, _, n = scales.shape
    words = np.ascontiguousarray(words).reshape(g, 128, n, -1)
    if fmt == "e4m3":
        vals = words.view(ml_dtypes.float8_e4m3fn).astype(np.float64)
    else:
        nib = np.empty((g, 128, n, 4), np.uint8)
        nib[..., 0::2] = words & 0xF
        nib[..., 1::2] = words >> 4
        vals = E2M1[nib]
    vals = vals * np.repeat(np.exp2(scales.astype(np.float64) - 127.0), 8, axis=1)[..., None]
    return vals.transpose(0, 1, 3, 2).reshape(g * 512, n)


def pack_table4(v):
    words, scales = pack_weight(v, "e2m1")
    g, t = words.shape[0] // 2, v.shape[1]
    words = words.reshape(g, 2, 128, t, 2).transpose(0, 2, 3, 1, 4)
    return np.concatenate([words.reshape(g, -1), scales.reshape(g, -1)], axis=1)


def unpack_table4(tab):
    g, t = tab.shape[0], tab.shape[1] // 544
    words = tab[:, :512 * t].reshape(g, 128, t, 2, 2).transpose(0, 3, 1, 2, 4).reshape(2 * g, 128, 2 * t)
    return unpack_weight(words, tab[:, 512 * t:].reshape(2 * g, 16, t), "e2m1")


K, M, T, S = 2048, 512, 4096, 1536


def setup_inputs():
    n = np.random.standard_normal
    s = mx_kscale(K)[:, None]
    return {
        "tab": pack_table4(n((K, T)) * s),
        "w": (n((K, M)) / np.sqrt(K) / s).astype(np.float32),
        "r": (n((512, 1536))).astype(np.float32),
        "offs": striped(np.random.permutation(T)[:S]),
    }


def reference(tab, w, r, offs):
    tab_ = unpack_table4(tab)[:, unstriped(offs)]
    w_ = mxq(f64(w), 0, "e4m3")
    y = w_.T @ tab_
    return f64(r) + y

@@ -1,0 +1,177 @@
+from contextlib import ExitStack
+
+import concourse.mybir as mybir
+
+K, M, T, S = 2048, 512, 4096, 1536
+FLOPS = 2 * K * M * S
+
+F32 = mybir.dt.float32
+BF16 = mybir.dt.bfloat16
+I32 = mybir.dt.int32
+U32 = mybir.dt.uint32
+U16 = mybir.dt.uint16
+U8 = mybir.dt.uint8
+E4M3X4 = mybir.dt.float8_e4m3fn_x4
+E2M1X4 = mybir.dt.float4_e2m1fn_x4
+ADD = mybir.AluOpType.add
+
+P = 128
+N = 512
+PASSES = 4
+PAIRS = 2
+NT = S // N
+MT = M // P
+
+
+def tile_list_tab4_res_kernel(tc, tab, w, r, offs, out):
+    nc = tc.nc
+    with ExitStack() as ctx:
+        keep = ctx.enter_context(tc.tile_pool(name="keep", bufs=1))
+        late_pool = ctx.enter_context(tc.tile_pool(name="late_pool", bufs=1))
+        psum = ctx.enter_context(tc.psum_pool(name="psum", bufs=8))
+
+        offsets = keep.tile([P, S // 16], U16, name="offsets")
+        scale_rows = late_pool.tile([P, T], U8, name="scale_rows", offset=4 * T - T // 2)
+        picked_rows = keep.tile([P, S], U8, name="picked_rows", align_bytes=64)
+        table0 = keep.tile([P, T], I32, name="table0", align_bytes=64)
+        w_first = [keep.tile([P, 4, M], F32, name=f"w_first{a}", align_bytes=64) for a in range(2)]
+        picked = [keep.tile([P, S], U32, name=f"picked{m}", align_bytes=64) for m in range(PAIRS)]
+        codes = [keep.tile([P, 4 * S], U8, name=f"codes{m}", align_bytes=64) for m in range(PAIRS)]
+        scales = [keep.tile([P, S], U8, name=f"scales{a}", align_bytes=64) for a in range(PASSES)]
+        w_bf = [keep.tile([P, M, 4], BF16, name=f"w_bf{a}", align_bytes=64) for a in range(PASSES)]
+        w_codes = [keep.tile([P, M], U32, name=f"w_codes{a}", align_bytes=64) for a in range(PASSES)]
+        w_scales = [keep.tile([P, M], U8, name=f"w_scales{a}", align_bytes=64) for a in range(PASSES)]
+
+        nc.gpsimd.memset(scale_rows[64:128, :].bitcast(I32), 0)
+        for a in range(PASSES):
+            nc.gpsimd.memset(scales[a][:].bitcast(I32), 0)
+        nc.sync.dma_start(out=offsets[:], in_=offs)
+        for m in range(PAIRS):
+            nc.sync.dma_start(
+                out=scale_rows[32 * m : 32 * m + 32, :].bitcast(I32),
+                in_=tab[m : m + 1, 512 * T : 544 * T].rearrange("o (q t) -> (o q) t", t=T).bitcast(I32),
+            )
+
+        def load_table(m):
+            nc.sync.dma_start(
+                out=table[m], in_=tab[m : m + 1, 0 : 512 * T].rearrange("o (p x) -> (o p) x", p=P).bitcast(I32)
+            )
+
+        def load_w(a):
+            nc.sync.dma_start(out=w_raw[a], in_=w[512 * a : 512 * (a + 1), :].rearrange("(p j) n -> p j n", j=4))
+
+        def load_r(view, first, width):
+            nc.sync.dma_start(out=view, in_=r[:, first : first + width].rearrange("(t p) j -> p t j", p=P))
+
+        def move(a):
+            for q in range(4):
+                nc.sync.dma_start(
+                    out=scales[a][32 * q : 32 * q + 4, :].bitcast(I32),
+                    in_=picked_rows[16 * a + 4 * q : 16 * a + 4 * q + 4, :].bitcast(I32),
+                )
+
+        table = [table0[:]]
+        w_raw = [t[:] for t in w_first]
+        load_table(0)
+        load_w(0)
+        load_w(1)
+
+        nc.vector.tensor_copy(picked_rows[:], scale_rows[:].indirect(offsets[:]))
+        table1 = late_pool.tile([P, T], I32, name="table1", offset=0)
+        late = late_pool.tile([P, 4 * 2 * M + MT * S], F32, name="late", offset=4 * T)
+        table.append(table1[:])
+        for i in range(2):
+            w_raw.append(late[:, 4 * M * i : 4 * M * (i + 1)].rearrange("p (j n) -> p j n", j=4))
+        r_first = 4 * 2 * M
+        r01 = late[:, r_first : r_first + MT * 2 * N].rearrange("p (t j) -> p t j", t=MT)
+        r2 = late[:, r_first + MT * 2 * N : r_first + MT * S].rearrange("p (t j) -> p t j", t=MT)
+        res = [r01[:, :, 0:N], r01[:, :, N : 2 * N], r2]
+
+        move(0)
+        load_table(1)
+        move(1)
+        load_w(2)
+        move(2)
+        load_w(3)
+        move(3)
+        load_r(r01, 0, 2 * N)
+        load_r(r2, 2 * N, N)
+
+        def gather(m, n):
+            nc.vector.tensor_copy(
+                picked[m][:, n * N : (n + 1) * N],
+                table[m].bitcast(U32).indirect(offsets[:, n * N // 16 : (n + 1) * N // 16]),
+            )
+
+        def part(m, n):
+            dst = codes[m][:].bitcast(U16).rearrange("p (h t) -> p h t", h=2)[:, :, n * N : (n + 1) * N]
+            src = picked[m][:, n * N : (n + 1) * N].bitcast(U16).rearrange("p (t h) -> p h t", h=2)
+            nc.vector.tensor_copy(dst, src)
+
+        def round_w(a):
+            if a < PASSES - 1:
+                nc.scalar.copy(w_bf[a][:], w_raw[a].rearrange("p j n -> p n j"))
+            else:
+                half = M // 2
+                nc.scalar.copy(w_bf[a][:, 0:half, :], w_raw[a][:, :, 0:half].rearrange("p j n -> p n j"))
+                nc.vector.tensor_copy(w_bf[a][:, half:M, :], w_raw[a][:, :, half:M].rearrange("p j n -> p n j"))
+
+        def quantize_w(a):
+            nc.vector.quantize_mx(
+                out=w_codes[a][:].bitcast(E4M3X4),
+                scales=w_scales[a][:],
+                in_=w_bf[a][:].rearrange("p n j -> p (n j)"),
+            )
+
+        def gather_pair(m):
+            gather(m, 0)
+            gather(m, 1)
+            part(m, 0)
+            gather(m, 2)
+            part(m, 1)
+            part(m, 2)
+
+        def multiply(bank, a, n, t):
+            base = 2 * S * (a % 2) + 2 * N * n
+            nc.tensor.matmul_mx(
+                out=bank[:],
+                lhsT=w_codes[a][:, t * P : (t + 1) * P].bitcast(E4M3X4),
+                lhsT_scale=w_scales[a][:, t * P : (t + 1) * P],
+                rhs=codes[a // 2][:, base : base + 2 * N].bitcast(E2M1X4),
+                rhs_scale=scales[a][:, n * N : (n + 1) * N],
+                start=(a == 0),
+                stop=(a == PASSES - 1),
+            )
+
+        def finish(bank, n, t):
+            nc.vector.tensor_tensor(out=res[n][:, t, :], in0=bank[:], in1=res[n][:, t, :], op=ADD)
+            nc.sync.dma_start(out=out[t * P : (t + 1) * P, n * N : (n + 1) * N], in_=res[n][:, t, :])
+
+        gather_pair(0)
+        round_w(0)
+        quantize_w(0)
+        round_w(1)
+        quantize_w(1)
+        early = [(n, t) for n in range(2) for t in range(MT)]
+        banks = {}
+        for n, t in early:
+            bank = psum.tile([P, N], F32, name="bank")
+            banks[(n, t)] = bank
+        for a in (0, 1):
+            for n, t in early:
+                multiply(banks[(n, t)], a, n, t)
+        gather_pair(1)
+        round_w(2)
+        quantize_w(2)
+        for n, t in early:
+            multiply(banks[(n, t)], 2, n, t)
+        round_w(3)
+        quantize_w(3)
+        for n, t in early:
+            multiply(banks[(n, t)], 3, n, t)
+            finish(banks[(n, t)], n, t)
+        for t in range(MT):
+            bank = psum.tile([P, N], F32, name="bank")
+            for a in range(PASSES):
+                multiply(bank, a, 2, t)
+            finish(bank, 2, t)

@@ -21,6 +21,9 @@ PASSES = 4
 PAIRS = 2
 NT = S // N
 MT = M // P
+HALVES = 2
+H = M // HALVES
+HT = MT // HALVES
 
 
 def tile_list_tab4_res_kernel(tc, tab, w, r, offs, out):
@@ -31,97 +34,90 @@ def tile_list_tab4_res_kernel(tc, tab, w, r, offs, out):
         psum = ctx.enter_context(tc.psum_pool(name="psum", bufs=8))
 
         offsets = keep.tile([P, S // 16], U16, name="offsets")
-        scale_rows = late_pool.tile([P, T], U8, name="scale_rows", offset=4 * T - T // 2)
         picked_rows = keep.tile([P, S], U8, name="picked_rows", align_bytes=64)
-        table0 = keep.tile([P, T], I32, name="table0", align_bytes=64)
-        w_first = [keep.tile([P, 4, M], F32, name=f"w_first{a}", align_bytes=64) for a in range(2)]
-        picked = [keep.tile([P, S], U32, name=f"picked{m}", align_bytes=64) for m in range(PAIRS)]
+        planes = keep.tile([P, PASSES * S], U8, name="planes", align_bytes=64)
+        table = [keep.tile([P, 4 * T], U8, name=f"table{m}", align_bytes=64) for m in range(PAIRS)]
+        scale_rows = table[1][:, 3 * T : 4 * T]
+        w_first = late_pool.tile([P, 4, H], F32, name="w_first", offset=0)
+        shared = ctx.enter_context(tc.tile_pool(name="shared", bufs=1))
+        picked = {}
         codes = [keep.tile([P, 4 * S], U8, name=f"codes{m}", align_bytes=64) for m in range(PAIRS)]
-        scales = [keep.tile([P, S], U8, name=f"scales{a}", align_bytes=64) for a in range(PASSES)]
-        w_bf = [keep.tile([P, M, 4], BF16, name=f"w_bf{a}", align_bytes=64) for a in range(PASSES)]
-        w_codes = [keep.tile([P, M], U32, name=f"w_codes{a}", align_bytes=64) for a in range(PASSES)]
-        w_scales = [keep.tile([P, M], U8, name=f"w_scales{a}", align_bytes=64) for a in range(PASSES)]
+        pieces = [(g, a) for g in range(HALVES) for a in range(PASSES)]
+        w_bf = {ga: keep.tile([P, H, 4], BF16, name="w_bf%d%d" % ga, align_bytes=64) for ga in pieces if ga != (0, 3)}
+        w_bf[(0, 3)] = shared.tile([P, H, 4], BF16, name="w_bf03", tag="turn", align_bytes=64)
+        w_codes = {ga: keep.tile([P, H], U32, name="w_codes%d%d" % ga, align_bytes=64) for ga in pieces}
+        w_scales = {ga: keep.tile([P, H], U8, name="w_scales%d%d" % ga, align_bytes=64) for ga in pieces}
 
-        nc.gpsimd.memset(scale_rows[64:128, :].bitcast(I32), 0)
-        for a in range(PASSES):
-            nc.gpsimd.memset(scales[a][:].bitcast(I32), 0)
+        nc.gpsimd.memset(table[1][64:128, 3 * T : 4 * T].bitcast(I32), 0)
+        nc.gpsimd.memset(planes[:].bitcast(I32), 0)
+
         nc.sync.dma_start(out=offsets[:], in_=offs)
         for m in range(PAIRS):
             nc.sync.dma_start(
-                out=scale_rows[32 * m : 32 * m + 32, :].bitcast(I32),
-                in_=tab[m : m + 1, 512 * T : 544 * T].rearrange("o (q t) -> (o q) t", t=T).bitcast(I32),
+                out=table[1][m:64:2, 3 * T : 4 * T].bitcast(I32),
+                in_=tab[m : m + 1, 512 * T : 544 * T].rearrange("o (h q t) -> (o q) h t", h=2, t=T).bitcast(I32),
             )
 
-        def load_table(m):
+        def load_table(m, first, last):
+            words = tab[m : m + 1, 0 : 512 * T].rearrange("o (p x) -> (o p) x", p=P)
+            nc.sync.dma_start(out=table[m][:, first:last].bitcast(I32), in_=words[:, first:last].bitcast(I32))
+
+        w_raw = {(0, 0): w_first[:]}
+
+        def load_w(g, a):
             nc.sync.dma_start(
-                out=table[m], in_=tab[m : m + 1, 0 : 512 * T].rearrange("o (p x) -> (o p) x", p=P).bitcast(I32)
+                out=w_raw[(g, a)],
+                in_=w[512 * a : 512 * (a + 1), g * H : (g + 1) * H].rearrange("(p j) n -> p j n", j=4),
             )
 
-        def load_w(a):
-            nc.sync.dma_start(out=w_raw[a], in_=w[512 * a : 512 * (a + 1), :].rearrange("(p j) n -> p j n", j=4))
+        load_table(0, 0, 4 * T)
+        load_w(0, 0)
+        load_table(1, 0, 2 * T)
 
-        def load_r(view, first, width):
-            nc.sync.dma_start(out=view, in_=r[:, first : first + width].rearrange("(t p) j -> p t j", p=P))
+        nc.vector.tensor_copy(picked_rows[:], scale_rows.indirect(offsets[:]))
+        for q in (0, 2, 1, 3):
+            nc.sync.dma_start(
+                out=planes[32 * q : 32 * q + 4, :].bitcast(I32).rearrange("p (c s) -> p c s", c=PASSES),
+                in_=picked_rows[16 * q : 16 * q + 16, :].bitcast(I32),
+            )
 
-        def move(a):
-            for q in range(4):
-                nc.sync.dma_start(
-                    out=scales[a][32 * q : 32 * q + 4, :].bitcast(I32),
-                    in_=picked_rows[16 * a + 4 * q : 16 * a + 4 * q + 4, :].bitcast(I32),
-                )
+        load_table(1, 2 * T, 4 * T)
 
-        table = [table0[:]]
-        w_raw = [t[:] for t in w_first]
-        load_table(0)
-        load_w(0)
-        load_w(1)
+        nc.scalar.copy(w_bf[(0, 0)][:], w_raw[(0, 0)].rearrange("p j n -> p n j"))
+        late = late_pool.tile([P, 7 * 4 * H + MT * S], F32, name="late", offset=0)
+        for i, ga in enumerate(pieces[1:]):
+            w_raw[ga] = late[:, 4 * H * i : 4 * H * (i + 1)].rearrange("p (j n) -> p j n", j=4)
+        r_first = 7 * 4 * H
+        res = [late[:, r_first + t * S : r_first + (t + 1) * S] for t in range(MT)]
 
-        nc.vector.tensor_copy(picked_rows[:], scale_rows[:].indirect(offsets[:]))
-        table1 = late_pool.tile([P, T], I32, name="table1", offset=0)
-        late = late_pool.tile([P, 4 * 2 * M + MT * S], F32, name="late", offset=4 * T)
-        table.append(table1[:])
-        for i in range(2):
-            w_raw.append(late[:, 4 * M * i : 4 * M * (i + 1)].rearrange("p (j n) -> p j n", j=4))
-        r_first = 4 * 2 * M
-        r01 = late[:, r_first : r_first + MT * 2 * N].rearrange("p (t j) -> p t j", t=MT)
-        r2 = late[:, r_first + MT * 2 * N : r_first + MT * S].rearrange("p (t j) -> p t j", t=MT)
-        res = [r01[:, :, 0:N], r01[:, :, N : 2 * N], r2]
+        def load_r(g):
+            nc.sync.dma_start(
+                out=late[:, r_first + g * HT * S : r_first + (g + 1) * HT * S].rearrange("p (t j) -> p t j", t=HT),
+                in_=r[g * H : (g + 1) * H, :].rearrange("(t p) j -> p t j", p=P),
+            )
 
-        move(0)
-        load_table(1)
-        move(1)
-        load_w(2)
-        move(2)
-        load_w(3)
-        move(3)
-        load_r(r01, 0, 2 * N)
-        load_r(r2, 2 * N, N)
+        for a in range(1, PASSES):
+            load_w(0, a)
+        load_w(1, 0)
+        load_r(0)
+        for a in range(1, PASSES):
+            load_w(1, a)
+        load_r(1)
 
         def gather(m, n):
+            if (m, n) == (1, 2):
+                picked[(m, n)] = shared.tile([P, N], U32, name="picked12", tag="turn", align_bytes=64)
+            else:
+                picked[(m, n)] = keep.tile([P, N], U32, name="picked%d%d" % (m, n), align_bytes=64)
             nc.vector.tensor_copy(
-                picked[m][:, n * N : (n + 1) * N],
-                table[m].bitcast(U32).indirect(offsets[:, n * N // 16 : (n + 1) * N // 16]),
+                picked[(m, n)][:],
+                table[m][:].bitcast(U32).indirect(offsets[:, n * N // 16 : (n + 1) * N // 16]),
             )
 
         def part(m, n):
             dst = codes[m][:].bitcast(U16).rearrange("p (h t) -> p h t", h=2)[:, :, n * N : (n + 1) * N]
-            src = picked[m][:, n * N : (n + 1) * N].bitcast(U16).rearrange("p (t h) -> p h t", h=2)
+            src = picked[(m, n)][:].bitcast(U16).rearrange("p (t h) -> p h t", h=2)
             nc.vector.tensor_copy(dst, src)
-
-        def round_w(a):
-            if a < PASSES - 1:
-                nc.scalar.copy(w_bf[a][:], w_raw[a].rearrange("p j n -> p n j"))
-            else:
-                half = M // 2
-                nc.scalar.copy(w_bf[a][:, 0:half, :], w_raw[a][:, :, 0:half].rearrange("p j n -> p n j"))
-                nc.vector.tensor_copy(w_bf[a][:, half:M, :], w_raw[a][:, :, half:M].rearrange("p j n -> p n j"))
-
-        def quantize_w(a):
-            nc.vector.quantize_mx(
-                out=w_codes[a][:].bitcast(E4M3X4),
-                scales=w_scales[a][:],
-                in_=w_bf[a][:].rearrange("p n j -> p (n j)"),
-            )
 
         def gather_pair(m):
             gather(m, 0)
@@ -131,47 +127,62 @@ def tile_list_tab4_res_kernel(tc, tab, w, r, offs, out):
             part(m, 1)
             part(m, 2)
 
+        def quantize_w(g, a):
+            if (g, a) != (0, 0):
+                nc.scalar.copy(w_bf[(g, a)][:], w_raw[(g, a)].rearrange("p j n -> p n j"))
+            nc.vector.quantize_mx(
+                out=w_codes[(g, a)][:].bitcast(E4M3X4),
+                scales=w_scales[(g, a)][:],
+                in_=w_bf[(g, a)][:].rearrange("p n j -> p (n j)"),
+            )
+
         def multiply(bank, a, n, t):
-            base = 2 * S * (a % 2) + 2 * N * n
+            g, u = divmod(t, HT)
+            m, h = divmod(a, 2)
+            base = 2 * S * h + 2 * N * n
+            plane = (2 * h + m) * S + n * N
             nc.tensor.matmul_mx(
                 out=bank[:],
-                lhsT=w_codes[a][:, t * P : (t + 1) * P].bitcast(E4M3X4),
-                lhsT_scale=w_scales[a][:, t * P : (t + 1) * P],
-                rhs=codes[a // 2][:, base : base + 2 * N].bitcast(E2M1X4),
-                rhs_scale=scales[a][:, n * N : (n + 1) * N],
+                lhsT=w_codes[(g, a)][:, u * P : (u + 1) * P].bitcast(E4M3X4),
+                lhsT_scale=w_scales[(g, a)][:, u * P : (u + 1) * P],
+                rhs=codes[m][:, base : base + 2 * N].bitcast(E2M1X4),
+                rhs_scale=planes[:, plane : plane + N],
                 start=(a == 0),
                 stop=(a == PASSES - 1),
             )
 
         def finish(bank, n, t):
-            nc.vector.tensor_tensor(out=res[n][:, t, :], in0=bank[:], in1=res[n][:, t, :], op=ADD)
-            nc.sync.dma_start(out=out[t * P : (t + 1) * P, n * N : (n + 1) * N], in_=res[n][:, t, :])
+            cols = slice(n * N, (n + 1) * N)
+            nc.vector.tensor_tensor(out=res[t][:, cols], in0=bank[:], in1=res[t][:, cols], op=ADD)
+            if n == NT - 1:
+                nc.sync.dma_start(out=out[t * P : (t + 1) * P, :], in_=res[t])
+
+        def sweep(g, tiles, between):
+            banks = {nt: psum.tile([P, N], F32, name="bank") for nt in tiles}
+            for a in (0, 1):
+                quantize_w(g, a)
+                for n, t in tiles:
+                    multiply(banks[(n, t)], a, n, t)
+            between()
+            for n, t in tiles:
+                multiply(banks[(n, t)], 2, n, t)
+                multiply(banks[(n, t)], 3, n, t)
+                finish(banks[(n, t)], n, t)
+
+        def second_pair():
+            gather(1, 0)
+            gather(1, 1)
+            part(1, 0)
+            part(1, 1)
+            quantize_w(0, 2)
+            quantize_w(0, 3)
+            gather(1, 2)
+            part(1, 2)
+
+        def last_weights():
+            quantize_w(1, 2)
+            quantize_w(1, 3)
 
         gather_pair(0)
-        round_w(0)
-        quantize_w(0)
-        round_w(1)
-        quantize_w(1)
-        early = [(n, t) for n in range(2) for t in range(MT)]
-        banks = {}
-        for n, t in early:
-            bank = psum.tile([P, N], F32, name="bank")
-            banks[(n, t)] = bank
-        for a in (0, 1):
-            for n, t in early:
-                multiply(banks[(n, t)], a, n, t)
-        gather_pair(1)
-        round_w(2)
-        quantize_w(2)
-        for n, t in early:
-            multiply(banks[(n, t)], 2, n, t)
-        round_w(3)
-        quantize_w(3)
-        for n, t in early:
-            multiply(banks[(n, t)], 3, n, t)
-            finish(banks[(n, t)], n, t)
-        for t in range(MT):
-            bank = psum.tile([P, N], F32, name="bank")
-            for a in range(PASSES):
-                multiply(bank, a, 2, t)
-            finish(bank, 2, t)
+        sweep(0, [(n, t) for n in range(NT) for t in range(HT)], second_pair)
+        sweep(1, [(n, t) for t in range(HT, MT) for n in range(NT)], last_weights)

@@ -21,94 +21,64 @@ PASSES = 4
 PAIRS = 2
 NT = S // N
 MT = M // P
-HALVES = 2
-H = M // HALVES
-HT = MT // HALVES
+H = M // 2
 
 
 def tile_list_tab4_res_kernel(tc, tab, w, r, offs, out):
     nc = tc.nc
     with ExitStack() as ctx:
         keep = ctx.enter_context(tc.tile_pool(name="keep", bufs=1))
-        late_pool = ctx.enter_context(tc.tile_pool(name="late_pool", bufs=1))
+        shared = ctx.enter_context(tc.tile_pool(name="shared", bufs=1))
         psum = ctx.enter_context(tc.psum_pool(name="psum", bufs=8))
 
         offsets = keep.tile([P, S // 16], U16, name="offsets")
+        scale_rows = keep.tile([P, T], U8, name="scale_rows", align_bytes=64)
         picked_rows = keep.tile([P, S], U8, name="picked_rows", align_bytes=64)
         planes = keep.tile([P, PASSES * S], U8, name="planes", align_bytes=64)
-        table = [keep.tile([P, 4 * T], U8, name=f"table{m}", align_bytes=64) for m in range(PAIRS)]
-        scale_rows = table[1][:, 3 * T : 4 * T]
-        w_first = late_pool.tile([P, 4, H], F32, name="w_first", offset=0)
-        shared = ctx.enter_context(tc.tile_pool(name="shared", bufs=1))
-        picked = {}
+        table = [keep.tile([P, T], I32, name=f"table{m}", align_bytes=64) for m in range(PAIRS)]
+        w_raw = [keep.tile([P, 4, M], F32, name=f"w_raw{a}", align_bytes=64) for a in range(PASSES)]
+        res = [keep.tile([P, S], F32, name=f"res{t}", align_bytes=64) for t in range(MT)]
         codes = [keep.tile([P, 4 * S], U8, name=f"codes{m}", align_bytes=64) for m in range(PAIRS)]
-        pieces = [(g, a) for g in range(HALVES) for a in range(PASSES)]
-        w_bf = {ga: keep.tile([P, H, 4], BF16, name="w_bf%d%d" % ga, align_bytes=64) for ga in pieces if ga != (0, 3)}
-        w_bf[(0, 3)] = shared.tile([P, H, 4], BF16, name="w_bf03", tag="turn", align_bytes=64)
-        w_codes = {ga: keep.tile([P, H], U32, name="w_codes%d%d" % ga, align_bytes=64) for ga in pieces}
-        w_scales = {ga: keep.tile([P, H], U8, name="w_scales%d%d" % ga, align_bytes=64) for ga in pieces}
+        w_codes = [keep.tile([P, M], U32, name=f"w_codes{a}", align_bytes=64) for a in range(PASSES)]
+        w_scales = [keep.tile([P, M], U8, name=f"w_scales{a}", align_bytes=64) for a in range(PASSES)]
+        picked = {}
+        w_bf = {}
 
-        nc.gpsimd.memset(table[1][64:128, 3 * T : 4 * T].bitcast(I32), 0)
+        nc.gpsimd.memset(scale_rows[64:128, :].bitcast(I32), 0)
         nc.gpsimd.memset(planes[:].bitcast(I32), 0)
 
         nc.sync.dma_start(out=offsets[:], in_=offs)
         for m in range(PAIRS):
             nc.sync.dma_start(
-                out=table[1][m:64:2, 3 * T : 4 * T].bitcast(I32),
+                out=scale_rows[m:64:2, :].bitcast(I32),
                 in_=tab[m : m + 1, 512 * T : 544 * T].rearrange("o (h q t) -> (o q) h t", h=2, t=T).bitcast(I32),
             )
 
-        def load_table(m, first, last):
+        def load_table(m):
             words = tab[m : m + 1, 0 : 512 * T].rearrange("o (p x) -> (o p) x", p=P)
-            nc.sync.dma_start(out=table[m][:, first:last].bitcast(I32), in_=words[:, first:last].bitcast(I32))
+            nc.sync.dma_start(out=table[m][:], in_=words.bitcast(I32))
 
-        w_raw = {(0, 0): w_first[:]}
+        def load_w(a):
+            nc.sync.dma_start(out=w_raw[a][:], in_=w[512 * a : 512 * (a + 1), :].rearrange("(p j) n -> p j n", j=4))
 
-        def load_w(g, a):
-            nc.sync.dma_start(
-                out=w_raw[(g, a)],
-                in_=w[512 * a : 512 * (a + 1), g * H : (g + 1) * H].rearrange("(p j) n -> p j n", j=4),
-            )
+        load_table(0)
+        load_w(0)
+        load_w(1)
+        load_table(1)
+        load_w(2)
+        load_w(3)
+        for t in range(MT):
+            nc.sync.dma_start(out=res[t][:], in_=r[t * P : (t + 1) * P, :])
 
-        load_table(0, 0, 4 * T)
-        load_w(0, 0)
-        load_table(1, 0, 2 * T)
-
-        nc.vector.tensor_copy(picked_rows[:], scale_rows.indirect(offsets[:]))
+        nc.vector.tensor_copy(picked_rows[:], scale_rows[:].indirect(offsets[:]))
         for q in (0, 2, 1, 3):
-            nc.sync.dma_start(
+            nc.gpsimd.dma_start(
                 out=planes[32 * q : 32 * q + 4, :].bitcast(I32).rearrange("p (c s) -> p c s", c=PASSES),
                 in_=picked_rows[16 * q : 16 * q + 16, :].bitcast(I32),
             )
 
-        load_table(1, 2 * T, 4 * T)
-
-        nc.scalar.copy(w_bf[(0, 0)][:], w_raw[(0, 0)].rearrange("p j n -> p n j"))
-        late = late_pool.tile([P, 7 * 4 * H + MT * S], F32, name="late", offset=0)
-        for i, ga in enumerate(pieces[1:]):
-            w_raw[ga] = late[:, 4 * H * i : 4 * H * (i + 1)].rearrange("p (j n) -> p j n", j=4)
-        r_first = 7 * 4 * H
-        res = [late[:, r_first + t * S : r_first + (t + 1) * S] for t in range(MT)]
-
-        def load_r(g):
-            nc.sync.dma_start(
-                out=late[:, r_first + g * HT * S : r_first + (g + 1) * HT * S].rearrange("p (t j) -> p t j", t=HT),
-                in_=r[g * H : (g + 1) * H, :].rearrange("(t p) j -> p t j", p=P),
-            )
-
-        for a in range(1, PASSES):
-            load_w(0, a)
-        load_w(1, 0)
-        load_r(0)
-        for a in range(1, PASSES):
-            load_w(1, a)
-        load_r(1)
-
-        def gather(m, n):
-            if (m, n) == (1, 2):
-                picked[(m, n)] = shared.tile([P, N], U32, name="picked12", tag="turn", align_bytes=64)
-            else:
-                picked[(m, n)] = keep.tile([P, N], U32, name="picked%d%d" % (m, n), align_bytes=64)
+        def gather(m, n, pool, tag):
+            picked[(m, n)] = pool.tile([P, N], U32, name="picked%d%d" % (m, n), tag=tag, align_bytes=64)
             nc.vector.tensor_copy(
                 picked[(m, n)][:],
                 table[m][:].bitcast(U32).indirect(offsets[:, n * N // 16 : (n + 1) * N // 16]),
@@ -119,32 +89,28 @@ def tile_list_tab4_res_kernel(tc, tab, w, r, offs, out):
             src = picked[(m, n)][:].bitcast(U16).rearrange("p (t h) -> p h t", h=2)
             nc.vector.tensor_copy(dst, src)
 
-        def gather_pair(m):
-            gather(m, 0)
-            gather(m, 1)
-            part(m, 0)
-            gather(m, 2)
-            part(m, 1)
-            part(m, 2)
+        def round_w(copy, a, first, last, pool, tag):
+            w_bf[(a, first)] = pool.tile([P, last - first, 4], BF16, name="w_bf%d_%d" % (a, first), tag=tag, align_bytes=64)
+            copy(
+                w_bf[(a, first)][:].rearrange("p (c i) j -> p c j i", i=4),
+                w_raw[a][:, :, first:last].rearrange("p j (c i) -> p c j i", i=4),
+            )
 
-        def quantize_w(g, a):
-            if (g, a) != (0, 0):
-                nc.scalar.copy(w_bf[(g, a)][:], w_raw[(g, a)].rearrange("p j n -> p n j"))
+        def quantize_w(a, first, last):
             nc.vector.quantize_mx(
-                out=w_codes[(g, a)][:].bitcast(E4M3X4),
-                scales=w_scales[(g, a)][:],
-                in_=w_bf[(g, a)][:].rearrange("p n j -> p (n j)"),
+                out=w_codes[a][:, first:last].bitcast(E4M3X4),
+                scales=w_scales[a][:, first:last],
+                in_=w_bf[(a, first)][:].rearrange("p n j -> p (n j)"),
             )
 
         def multiply(bank, a, n, t):
-            g, u = divmod(t, HT)
             m, h = divmod(a, 2)
             base = 2 * S * h + 2 * N * n
             plane = (2 * h + m) * S + n * N
             nc.tensor.matmul_mx(
                 out=bank[:],
-                lhsT=w_codes[(g, a)][:, u * P : (u + 1) * P].bitcast(E4M3X4),
-                lhsT_scale=w_scales[(g, a)][:, u * P : (u + 1) * P],
+                lhsT=w_codes[a][:, t * P : (t + 1) * P].bitcast(E4M3X4),
+                lhsT_scale=w_scales[a][:, t * P : (t + 1) * P],
                 rhs=codes[m][:, base : base + 2 * N].bitcast(E2M1X4),
                 rhs_scale=planes[:, plane : plane + N],
                 start=(a == 0),
@@ -154,35 +120,49 @@ def tile_list_tab4_res_kernel(tc, tab, w, r, offs, out):
         def finish(bank, n, t):
             cols = slice(n * N, (n + 1) * N)
             nc.vector.tensor_tensor(out=res[t][:, cols], in0=bank[:], in1=res[t][:, cols], op=ADD)
-            if n == NT - 1:
-                nc.sync.dma_start(out=out[t * P : (t + 1) * P, :], in_=res[t])
+            rows = slice(t * P, (t + 1) * P)
+            if t < MT - 1 and n == NT - 1:
+                nc.sync.dma_start(out=out[rows, :], in_=res[t][:])
+            if t == MT - 1 and n == NT - 2:
+                nc.sync.dma_start(out=out[rows, 0 : 2 * N], in_=res[t][:, 0 : 2 * N])
+            if t == MT - 1 and n == NT - 1:
+                nc.sync.dma_start(out=out[rows, cols], in_=res[t][:, cols])
 
-        def sweep(g, tiles, between):
-            banks = {nt: psum.tile([P, N], F32, name="bank") for nt in tiles}
-            for a in (0, 1):
-                quantize_w(g, a)
-                for n, t in tiles:
-                    multiply(banks[(n, t)], a, n, t)
-            between()
-            for n, t in tiles:
-                multiply(banks[(n, t)], 2, n, t)
-                multiply(banks[(n, t)], 3, n, t)
-                finish(banks[(n, t)], n, t)
-
-        def second_pair():
-            gather(1, 0)
-            gather(1, 1)
-            part(1, 0)
-            part(1, 1)
-            quantize_w(0, 2)
-            quantize_w(0, 3)
-            gather(1, 2)
-            part(1, 2)
-
-        def last_weights():
-            quantize_w(1, 2)
-            quantize_w(1, 3)
-
-        gather_pair(0)
-        sweep(0, [(n, t) for n in range(NT) for t in range(HT)], second_pair)
-        sweep(1, [(n, t) for t in range(HT, MT) for n in range(NT)], last_weights)
+        gather(0, 0, keep, "p00")
+        gather(0, 1, keep, "p01")
+        part(0, 0)
+        gather(0, 2, keep, "p02")
+        part(0, 1)
+        part(0, 2)
+        tiles = [(n, t) for t in range(MT) for n in range(NT)]
+        early, late = tiles[:8], tiles[8:]
+        banks = {nt: psum.tile([P, N], F32, name="bank") for nt in early}
+        for a in (0, 1):
+            round_w(nc.scalar.copy, a, 0, M, keep, f"b{a}")
+            quantize_w(a, 0, M)
+            for n, t in early:
+                multiply(banks[(n, t)], a, n, t)
+        gather(1, 0, keep, "p10")
+        gather(1, 1, keep, "p11")
+        part(1, 0)
+        part(1, 1)
+        round_w(nc.scalar.copy, 2, 0, H, shared, "turn")
+        quantize_w(2, 0, H)
+        gather(1, 2, shared, "turn")
+        part(1, 2)
+        round_w(nc.scalar.copy, 2, H, M, keep, "b2")
+        quantize_w(2, H, M)
+        for n, t in sorted(early, key=lambda nt: (nt[1] // 2, nt[0])):
+            multiply(banks[(n, t)], 2, n, t)
+        round_w(nc.scalar.copy, 3, 0, H, keep, "b3")
+        round_w(nc.vector.tensor_copy, 3, H, M, keep, "b4")
+        quantize_w(3, 0, H)
+        quantize_w(3, H, M)
+        for n, t in early:
+            multiply(banks[(n, t)], 3, n, t)
+            finish(banks[(n, t)], n, t)
+        for n, t in late:
+            bank = psum.tile([P, N], F32, name="bank")
+            for a in range(PASSES):
+                multiply(bank, a, n, t)
+            finish(bank, n, t)

@@ -29,15 +29,15 @@ def tile_list_tab4_res_kernel(tc, tab, w, r, offs, out):
     with ExitStack() as ctx:
         keep = ctx.enter_context(tc.tile_pool(name="keep", bufs=1))
         shared = ctx.enter_context(tc.tile_pool(name="shared", bufs=1))
+        late_pool = ctx.enter_context(tc.tile_pool(name="late_pool", bufs=1))
         psum = ctx.enter_context(tc.psum_pool(name="psum", bufs=8))
 
         offsets = keep.tile([P, S // 16], U16, name="offsets")
-        scale_rows = keep.tile([P, T], U8, name="scale_rows", align_bytes=64)
+        scale_rows = late_pool.tile([P, T], U8, name="scale_rows", offset=4 * T - T // 2)
         picked_rows = keep.tile([P, S], U8, name="picked_rows", align_bytes=64)
-        planes = keep.tile([P, PASSES * S], U8, name="planes", align_bytes=64)
-        table = [keep.tile([P, T], I32, name=f"table{m}", align_bytes=64) for m in range(PAIRS)]
-        w_raw = [keep.tile([P, 4, M], F32, name=f"w_raw{a}", align_bytes=64) for a in range(PASSES)]
-        res = [keep.tile([P, S], F32, name=f"res{t}", align_bytes=64) for t in range(MT)]
+        planes = [keep.tile([P, PAIRS * S], U8, name=f"planes{h}", align_bytes=64) for h in range(2)]
+        table = [keep.tile([P, T], I32, name="table0", align_bytes=64)[:]]
+        w_raw = [keep.tile([P, 4, M], F32, name=f"w_raw{a}", align_bytes=64)[:] for a in range(2)]
         codes = [keep.tile([P, 4 * S], U8, name=f"codes{m}", align_bytes=64) for m in range(PAIRS)]
         w_codes = [keep.tile([P, M], U32, name=f"w_codes{a}", align_bytes=64) for a in range(PASSES)]
         w_scales = [keep.tile([P, M], U8, name=f"w_scales{a}", align_bytes=64) for a in range(PASSES)]
@@ -45,43 +45,53 @@ def tile_list_tab4_res_kernel(tc, tab, w, r, offs, out):
         w_bf = {}
 
         nc.gpsimd.memset(scale_rows[64:128, :].bitcast(I32), 0)
-        nc.gpsimd.memset(planes[:].bitcast(I32), 0)
+        for h in range(2):
+            nc.gpsimd.memset(planes[h][:].bitcast(I32), 0)
 
         nc.sync.dma_start(out=offsets[:], in_=offs)
-        for m in range(PAIRS):
-            nc.sync.dma_start(
-                out=scale_rows[m:64:2, :].bitcast(I32),
-                in_=tab[m : m + 1, 512 * T : 544 * T].rearrange("o (h q t) -> (o q) h t", h=2, t=T).bitcast(I32),
-            )
+        by_row = tab[:, 512 * T : 544 * T].rearrange("m (x i t) -> i x m t", i=4, t=T)
+        for i in range(4):
+            nc.sync.dma_start(out=scale_rows[i:64:4, :].bitcast(I32), in_=by_row[i].bitcast(I32))
 
         def load_table(m):
             words = tab[m : m + 1, 0 : 512 * T].rearrange("o (p x) -> (o p) x", p=P)
-            nc.sync.dma_start(out=table[m][:], in_=words.bitcast(I32))
+            nc.sync.dma_start(out=table[m], in_=words.bitcast(I32))
 
         def load_w(a):
-            nc.sync.dma_start(out=w_raw[a][:], in_=w[512 * a : 512 * (a + 1), :].rearrange("(p j) n -> p j n", j=4))
+            nc.sync.dma_start(out=w_raw[a], in_=w[512 * a : 512 * (a + 1), :].rearrange("(p j) n -> p j n", j=4))
 
         load_table(0)
         load_w(0)
         load_w(1)
+
+        nc.vector.tensor_copy(picked_rows[:], scale_rows[:].indirect(offsets[:]))
+
+        def move(h):
+            for i in range(4):
+                nc.sync.dma_start(
+                    out=planes[h][i:128:32, :].bitcast(I32).rearrange("p (m s) -> p m s", m=2),
+                    in_=picked_rows[32 * h + i : 32 * h + 32 : 4, :].bitcast(I32),
+                )
+
+        move(0)
+
+        table.append(late_pool.tile([P, T], I32, name="table1", offset=0)[:])
+        later = late_pool.tile([P, 2 * 4 * M + MT * S], F32, name="later", offset=4 * T)
+        for i in range(2):
+            w_raw.append(later[:, 4 * M * i : 4 * M * (i + 1)].rearrange("p (j n) -> p j n", j=4))
+        res = [later[:, 8 * M + t * S : 8 * M + (t + 1) * S] for t in range(MT)]
         load_table(1)
+        move(1)
         load_w(2)
         load_w(3)
         for t in range(MT):
-            nc.sync.dma_start(out=res[t][:], in_=r[t * P : (t + 1) * P, :])
-
-        nc.vector.tensor_copy(picked_rows[:], scale_rows[:].indirect(offsets[:]))
-        for q in (0, 2, 1, 3):
-            nc.gpsimd.dma_start(
-                out=planes[32 * q : 32 * q + 4, :].bitcast(I32).rearrange("p (c s) -> p c s", c=PASSES),
-                in_=picked_rows[16 * q : 16 * q + 16, :].bitcast(I32),
-            )
+            nc.sync.dma_start(out=res[t], in_=r[t * P : (t + 1) * P, :])
 
         def gather(m, n, pool, tag):
             picked[(m, n)] = pool.tile([P, N], U32, name="picked%d%d" % (m, n), tag=tag, align_bytes=64)
             nc.vector.tensor_copy(
                 picked[(m, n)][:],
-                table[m][:].bitcast(U32).indirect(offsets[:, n * N // 16 : (n + 1) * N // 16]),
+                table[m].bitcast(U32).indirect(offsets[:, n * N // 16 : (n + 1) * N // 16]),
             )
 
         def part(m, n):
@@ -106,13 +116,13 @@ def tile_list_tab4_res_kernel(tc, tab, w, r, offs, out):
         def multiply(bank, a, n, t):
             m, h = divmod(a, 2)
             base = 2 * S * h + 2 * N * n
-            plane = (2 * h + m) * S + n * N
+            plane = m * S + n * N
             nc.tensor.matmul_mx(
                 out=bank[:],
                 lhsT=w_codes[a][:, t * P : (t + 1) * P].bitcast(E4M3X4),
                 lhsT_scale=w_scales[a][:, t * P : (t + 1) * P],
                 rhs=codes[m][:, base : base + 2 * N].bitcast(E2M1X4),
-                rhs_scale=planes[:, plane : plane + N],
+                rhs_scale=planes[h][:, plane : plane + N],
                 start=(a == 0),
                 stop=(a == PASSES - 1),
             )
@@ -122,7 +132,7 @@ def tile_list_tab4_res_kernel(tc, tab, w, r, offs, out):
             nc.vector.tensor_tensor(out=res[t][:, cols], in0=bank[:], in1=res[t][:, cols], op=ADD)
             rows = slice(t * P, (t + 1) * P)
             if t < MT - 1 and n == NT - 1:
-                nc.sync.dma_start(out=out[rows, :], in_=res[t][:])
+                nc.sync.dma_start(out=out[rows, :], in_=res[t])
             if t == MT - 1 and n == NT - 2:
                 nc.sync.dma_start(out=out[rows, 0 : 2 * N], in_=res[t][:, 0 : 2 * N])
             if t == MT - 1 and n == NT - 1:
@@ -155,8 +165,8 @@ def tile_list_tab4_res_kernel(tc, tab, w, r, offs, out):
         for n, t in sorted(early, key=lambda nt: (nt[1] // 2, nt[0])):
             multiply(banks[(n, t)], 2, n, t)
         round_w(nc.scalar.copy, 3, 0, H, keep, "b3")
-        round_w(nc.vector.tensor_copy, 3, H, M, keep, "b4")
         quantize_w(3, 0, H)
+        round_w(nc.scalar.copy, 3, H, M, keep, "b4")
         quantize_w(3, H, M)
         for n, t in early:
             multiply(banks[(n, t)], 3, n, t)

@@ -35,23 +35,24 @@ def tile_list_tab4_res_kernel(tc, tab, w, r, offs, out):
         offsets = keep.tile([P, S // 16], U16, name="offsets")
         scale_rows = late_pool.tile([P, T], U8, name="scale_rows", offset=4 * T - T // 2)
         picked_rows = keep.tile([P, S], U8, name="picked_rows", align_bytes=64)
-        planes = [keep.tile([P, PAIRS * S], U8, name=f"planes{h}", align_bytes=64) for h in range(2)]
+        planes = keep.tile([P, PASSES * S], U8, name="planes", align_bytes=64)
         table = [keep.tile([P, T], I32, name="table0", align_bytes=64)[:]]
         w_raw = [keep.tile([P, 4, M], F32, name=f"w_raw{a}", align_bytes=64)[:] for a in range(2)]
-        codes = [keep.tile([P, 4 * S], U8, name=f"codes{m}", align_bytes=64) for m in range(PAIRS)]
         w_codes = [keep.tile([P, M], U32, name=f"w_codes{a}", align_bytes=64) for a in range(PASSES)]
         w_scales = [keep.tile([P, M], U8, name=f"w_scales{a}", align_bytes=64) for a in range(PASSES)]
         picked = {}
+        codes = {}
         w_bf = {}
 
         nc.gpsimd.memset(scale_rows[64:128, :].bitcast(I32), 0)
-        for h in range(2):
-            nc.gpsimd.memset(planes[h][:].bitcast(I32), 0)
+        nc.gpsimd.memset(planes[:].bitcast(I32), 0)
 
         nc.sync.dma_start(out=offsets[:], in_=offs)
-        by_row = tab[:, 512 * T : 544 * T].rearrange("m (x i t) -> i x m t", i=4, t=T)
-        for i in range(4):
-            nc.sync.dma_start(out=scale_rows[i:64:4, :].bitcast(I32), in_=by_row[i].bitcast(I32))
+        for m in range(PAIRS):
+            nc.sync.dma_start(
+                out=scale_rows[m:64:2, :].bitcast(I32),
+                in_=tab[m : m + 1, 512 * T : 544 * T].rearrange("o (h q t) -> (o q) h t", h=2, t=T).bitcast(I32),
+            )
 
         def load_table(m):
             words = tab[m : m + 1, 0 : 512 * T].rearrange("o (p x) -> (o p) x", p=P)
@@ -65,15 +66,11 @@ def tile_list_tab4_res_kernel(tc, tab, w, r, offs, out):
         load_w(1)
 
         nc.vector.tensor_copy(picked_rows[:], scale_rows[:].indirect(offsets[:]))
-
-        def move(h):
-            for i in range(4):
-                nc.sync.dma_start(
-                    out=planes[h][i:128:32, :].bitcast(I32).rearrange("p (m s) -> p m s", m=2),
-                    in_=picked_rows[32 * h + i : 32 * h + 32 : 4, :].bitcast(I32),
-                )
-
-        move(0)
+        for q in (0, 2, 1, 3):
+            nc.sync.dma_start(
+                out=planes[32 * q : 32 * q + 4, :].bitcast(I32).rearrange("p (c s) -> p c s", c=PASSES),
+                in_=picked_rows[16 * q : 16 * q + 16, :].bitcast(I32),
+            )
 
         table.append(late_pool.tile([P, T], I32, name="table1", offset=0)[:])
         later = late_pool.tile([P, 2 * 4 * M + MT * S], F32, name="later", offset=4 * T)
@@ -81,7 +78,6 @@ def tile_list_tab4_res_kernel(tc, tab, w, r, offs, out):
             w_raw.append(later[:, 4 * M * i : 4 * M * (i + 1)].rearrange("p (j n) -> p j n", j=4))
         res = [later[:, 8 * M + t * S : 8 * M + (t + 1) * S] for t in range(MT)]
         load_table(1)
-        move(1)
         load_w(2)
         load_w(3)
         for t in range(MT):
@@ -94,8 +90,9 @@ def tile_list_tab4_res_kernel(tc, tab, w, r, offs, out):
                 table[m].bitcast(U32).indirect(offsets[:, n * N // 16 : (n + 1) * N // 16]),
             )
 
-        def part(m, n):
-            dst = codes[m][:].bitcast(U16).rearrange("p (h t) -> p h t", h=2)[:, :, n * N : (n + 1) * N]
+        def part(m, n, pool, tag):
+            codes[(m, n)] = pool.tile([P, 4 * N], U8, name="codes%d%d" % (m, n), tag=tag, align_bytes=64)
+            dst = codes[(m, n)][:].bitcast(U16).rearrange("p (h t) -> p h t", h=2)
             src = picked[(m, n)][:].bitcast(U16).rearrange("p (t h) -> p h t", h=2)
             nc.vector.tensor_copy(dst, src)
 
@@ -115,14 +112,13 @@ def tile_list_tab4_res_kernel(tc, tab, w, r, offs, out):
 
         def multiply(bank, a, n, t):
             m, h = divmod(a, 2)
-            base = 2 * S * h + 2 * N * n
-            plane = m * S + n * N
+            plane = (2 * h + m) * S + n * N
             nc.tensor.matmul_mx(
                 out=bank[:],
                 lhsT=w_codes[a][:, t * P : (t + 1) * P].bitcast(E4M3X4),
                 lhsT_scale=w_scales[a][:, t * P : (t + 1) * P],
-                rhs=codes[m][:, base : base + 2 * N].bitcast(E2M1X4),
-                rhs_scale=planes[h][:, plane : plane + N],
+                rhs=codes[(m, n)][:, 2 * N * h : 2 * N * (h + 1)].bitcast(E2M1X4),
+                rhs_scale=planes[:, plane : plane + N],
                 start=(a == 0),
                 stop=(a == PASSES - 1),
             )
@@ -130,20 +126,15 @@ def tile_list_tab4_res_kernel(tc, tab, w, r, offs, out):
         def finish(bank, n, t):
             cols = slice(n * N, (n + 1) * N)
             nc.vector.tensor_tensor(out=res[t][:, cols], in0=bank[:], in1=res[t][:, cols], op=ADD)
-            rows = slice(t * P, (t + 1) * P)
-            if t < MT - 1 and n == NT - 1:
-                nc.sync.dma_start(out=out[rows, :], in_=res[t])
-            if t == MT - 1 and n == NT - 2:
-                nc.sync.dma_start(out=out[rows, 0 : 2 * N], in_=res[t][:, 0 : 2 * N])
-            if t == MT - 1 and n == NT - 1:
-                nc.sync.dma_start(out=out[rows, cols], in_=res[t][:, cols])
+            if n == NT - 1:
+                nc.sync.dma_start(out=out[t * P : (t + 1) * P, :], in_=res[t])
 
         gather(0, 0, keep, "p00")
         gather(0, 1, keep, "p01")
-        part(0, 0)
+        part(0, 0, keep, "c00")
         gather(0, 2, keep, "p02")
-        part(0, 1)
-        part(0, 2)
+        part(0, 1, keep, "c01")
+        part(0, 2, keep, "c02")
         tiles = [(n, t) for t in range(MT) for n in range(NT)]
         early, late = tiles[:8], tiles[8:]
         banks = {nt: psum.tile([P, N], F32, name="bank") for nt in early}
@@ -154,19 +145,19 @@ def tile_list_tab4_res_kernel(tc, tab, w, r, offs, out):
                 multiply(banks[(n, t)], a, n, t)
         gather(1, 0, keep, "p10")
         gather(1, 1, keep, "p11")
-        part(1, 0)
-        part(1, 1)
-        round_w(nc.scalar.copy, 2, 0, H, shared, "turn")
+        part(1, 0, keep, "c10")
+        part(1, 1, keep, "c11")
+        round_w(nc.scalar.copy, 2, 0, H, shared, "turn2")
         quantize_w(2, 0, H)
-        gather(1, 2, shared, "turn")
-        part(1, 2)
-        round_w(nc.scalar.copy, 2, H, M, keep, "b2")
+        gather(1, 2, shared, "turn2")
+        round_w(nc.scalar.copy, 2, H, M, shared, "turn3")
         quantize_w(2, H, M)
-        for n, t in sorted(early, key=lambda nt: (nt[1] // 2, nt[0])):
+        part(1, 2, shared, "turn3")
+        for n, t in sorted(early, key=lambda nt: (nt[0] // 2, nt[1])):
             multiply(banks[(n, t)], 2, n, t)
-        round_w(nc.scalar.copy, 3, 0, H, keep, "b3")
+        round_w(nc.scalar.copy, 3, 0, H, keep, "b2")
         quantize_w(3, 0, H)
-        round_w(nc.scalar.copy, 3, H, M, keep, "b4")
+        round_w(nc.scalar.copy, 3, H, M, keep, "b3")
         quantize_w(3, H, M)
         for n, t in early:
             multiply(banks[(n, t)], 3, n, t)

@@ -28,29 +28,29 @@ def tile_list_tab4_res_kernel(tc, tab, w, r, offs, out):
     nc = tc.nc
     with ExitStack() as ctx:
         keep = ctx.enter_context(tc.tile_pool(name="keep", bufs=1))
-        shared = ctx.enter_context(tc.tile_pool(name="shared", bufs=1))
         late_pool = ctx.enter_context(tc.tile_pool(name="late_pool", bufs=1))
         psum = ctx.enter_context(tc.psum_pool(name="psum", bufs=8))
 
         offsets = keep.tile([P, S // 16], U16, name="offsets")
-        scale_rows = late_pool.tile([P, T], U8, name="scale_rows", offset=4 * T - T // 2)
+        scale_rows = late_pool.tile([P, T], U8, name="scale_rows", offset=0)
         picked_rows = keep.tile([P, S], U8, name="picked_rows", align_bytes=64)
         planes = keep.tile([P, PASSES * S], U8, name="planes", align_bytes=64)
-        table = [keep.tile([P, T], I32, name="table0", align_bytes=64)[:]]
-        w_raw = [keep.tile([P, 4, M], F32, name=f"w_raw{a}", align_bytes=64)[:] for a in range(2)]
+        table = [keep.tile([P, T], I32, name=f"table{m}", align_bytes=64)[:] for m in range(PAIRS)]
+        w_raw = [keep.tile([P, 4, M], F32, name="w_raw0", align_bytes=64)[:]]
         w_codes = [keep.tile([P, M], U32, name=f"w_codes{a}", align_bytes=64) for a in range(PASSES)]
         w_scales = [keep.tile([P, M], U8, name=f"w_scales{a}", align_bytes=64) for a in range(PASSES)]
         picked = {}
         codes = {}
         w_bf = {}
 
-        nc.gpsimd.memset(scale_rows[64:128, :].bitcast(I32), 0)
-        nc.gpsimd.memset(planes[:].bitcast(I32), 0)
+        nc.gpsimd.memset(scale_rows[0:32, :].bitcast(I32), 0)
+        nc.gpsimd.memset(scale_rows[96:128, :].bitcast(I32), 0)
+        nc.vector.memset(planes[:].bitcast(I32), 0)
 
         nc.sync.dma_start(out=offsets[:], in_=offs)
         for m in range(PAIRS):
             nc.sync.dma_start(
-                out=scale_rows[m:64:2, :].bitcast(I32),
+                out=scale_rows[32 + m : 96 : 2, :].bitcast(I32),
                 in_=tab[m : m + 1, 512 * T : 544 * T].rearrange("o (h q t) -> (o q) h t", h=2, t=T).bitcast(I32),
             )
 
@@ -63,23 +63,21 @@ def tile_list_tab4_res_kernel(tc, tab, w, r, offs, out):
 
         load_table(0)
         load_w(0)
-        load_w(1)
+        load_table(1)
 
         nc.vector.tensor_copy(picked_rows[:], scale_rows[:].indirect(offsets[:]))
         for q in (0, 2, 1, 3):
             nc.sync.dma_start(
                 out=planes[32 * q : 32 * q + 4, :].bitcast(I32).rearrange("p (c s) -> p c s", c=PASSES),
-                in_=picked_rows[16 * q : 16 * q + 16, :].bitcast(I32),
+                in_=picked_rows[32 + 16 * q : 48 + 16 * q, :].bitcast(I32),
             )
 
-        table.append(late_pool.tile([P, T], I32, name="table1", offset=0)[:])
-        later = late_pool.tile([P, 2 * 4 * M + MT * S], F32, name="later", offset=4 * T)
-        for i in range(2):
+        later = late_pool.tile([P, 3 * 4 * M + MT * S], F32, name="later", offset=0)
+        for i in range(3):
             w_raw.append(later[:, 4 * M * i : 4 * M * (i + 1)].rearrange("p (j n) -> p j n", j=4))
-        res = [later[:, 8 * M + t * S : 8 * M + (t + 1) * S] for t in range(MT)]
-        load_table(1)
-        load_w(2)
-        load_w(3)
+        res = [later[:, 12 * M + t * S : 12 * M + (t + 1) * S] for t in range(MT)]
+        for a in range(1, PASSES):
+            load_w(a)
         for t in range(MT):
             nc.sync.dma_start(out=res[t], in_=r[t * P : (t + 1) * P, :])
 
@@ -126,8 +124,20 @@ def tile_list_tab4_res_kernel(tc, tab, w, r, offs, out):
         def finish(bank, n, t):
             cols = slice(n * N, (n + 1) * N)
             nc.vector.tensor_tensor(out=res[t][:, cols], in0=bank[:], in1=res[t][:, cols], op=ADD)
-            if n == NT - 1:
+            if t == MT - 1:
+                nc.sync.dma_start(out=out[t * P : (t + 1) * P, cols], in_=res[t][:, cols])
+            elif n == NT - 1:
                 nc.sync.dma_start(out=out[t * P : (t + 1) * P, :], in_=res[t])
+
+        tiles = [(n, t) for t in range(MT) for n in range(NT)]
+        early, late = tiles[:8], tiles[8:]
+        banks = {nt: psum.tile([P, N], F32, name="bank") for nt in early}
+
+        def early_pass(a):
+            for n, t in early:
+                multiply(banks[(n, t)], a, n, t)
+                if a == PASSES - 1:
+                    finish(banks[(n, t)], n, t)
 
         gather(0, 0, keep, "p00")
         gather(0, 1, keep, "p01")
@@ -135,33 +145,28 @@ def tile_list_tab4_res_kernel(tc, tab, w, r, offs, out):
         gather(0, 2, keep, "p02")
         part(0, 1, keep, "c01")
         part(0, 2, keep, "c02")
-        tiles = [(n, t) for t in range(MT) for n in range(NT)]
-        early, late = tiles[:8], tiles[8:]
-        banks = {nt: psum.tile([P, N], F32, name="bank") for nt in early}
-        for a in (0, 1):
-            round_w(nc.scalar.copy, a, 0, M, keep, f"b{a}")
-            quantize_w(a, 0, M)
-            for n, t in early:
-                multiply(banks[(n, t)], a, n, t)
-        gather(1, 0, keep, "p10")
-        gather(1, 1, keep, "p11")
+        for first in (0, H):
+            round_w(nc.scalar.copy, 0, first, first + H, keep, f"b0{first}")
+            quantize_w(0, first, first + H)
+        early_pass(0)
+        for n in range(NT):
+            gather(1, n, keep, f"p1{n}")
         part(1, 0, keep, "c10")
-        part(1, 1, keep, "c11")
-        round_w(nc.scalar.copy, 2, 0, H, shared, "turn2")
-        quantize_w(2, 0, H)
-        gather(1, 2, shared, "turn2")
-        round_w(nc.scalar.copy, 2, H, M, shared, "turn3")
-        quantize_w(2, H, M)
-        part(1, 2, shared, "turn3")
-        for n, t in sorted(early, key=lambda nt: (nt[0] // 2, nt[1])):
-            multiply(banks[(n, t)], 2, n, t)
-        round_w(nc.scalar.copy, 3, 0, H, keep, "b2")
+        for first, last, tag in ((0, P, "turn1"), (P, H, "turn2"), (H, M, "b1")):
+            round_w(nc.scalar.copy, 1, first, last, keep, tag)
+            quantize_w(1, first, last)
+        early_pass(1)
+        part(1, 1, keep, "turn1")
+        part(1, 2, keep, "turn2")
+        for first, last in ((0, P), (P, H), (H, M)):
+            round_w(nc.scalar.copy, 2, first, last, keep, f"b2{first}")
+            quantize_w(2, first, last)
+        early_pass(2)
+        round_w(nc.vector.tensor_copy, 3, 0, H, keep, "b30")
+        round_w(nc.scalar.copy, 3, H, M, keep, "b31")
         quantize_w(3, 0, H)
-        round_w(nc.scalar.copy, 3, H, M, keep, "b3")
         quantize_w(3, H, M)
-        for n, t in early:
-            multiply(banks[(n, t)], 3, n, t)
-            finish(banks[(n, t)], n, t)
+        early_pass(3)
         for n, t in late:
             bank = psum.tile([P, N], F32, name="bank")
             for a in range(PASSES):

@@ -32,11 +32,11 @@ def tile_list_tab4_res_kernel(tc, tab, w, r, offs, out):
         psum = ctx.enter_context(tc.psum_pool(name="psum", bufs=8))
 
         offsets = keep.tile([P, S // 16], U16, name="offsets")
-        scale_rows = late_pool.tile([P, T], U8, name="scale_rows", offset=0)
-        picked_rows = keep.tile([P, S], U8, name="picked_rows", align_bytes=64)
-        planes = keep.tile([P, PASSES * S], U8, name="planes", align_bytes=64)
-        table = [keep.tile([P, T], I32, name=f"table{m}", align_bytes=64)[:] for m in range(PAIRS)]
-        w_raw = [keep.tile([P, 4, M], F32, name="w_raw0", align_bytes=64)[:]]
+        scale_rows = late_pool.tile([P, T], U8, name="scale_rows", offset=0, align_bytes=256)
+        picked_rows = keep.tile([P, S], U8, name="picked_rows", align_bytes=256)
+        planes = keep.tile([P, PASSES * S], U8, name="planes", align_bytes=256)
+        table = [keep.tile([P, T], I32, name=f"table{m}", align_bytes=256)[:] for m in range(PAIRS)]
+        w_raw = [keep.tile([P, 4, M], F32, name="w_raw0", align_bytes=256)[:]]
         w_codes = [keep.tile([P, M], U32, name=f"w_codes{a}", align_bytes=64) for a in range(PASSES)]
         w_scales = [keep.tile([P, M], U8, name=f"w_scales{a}", align_bytes=64) for a in range(PASSES)]
         picked = {}
@@ -72,7 +72,7 @@ def tile_list_tab4_res_kernel(tc, tab, w, r, offs, out):
                 in_=picked_rows[32 + 16 * q : 48 + 16 * q, :].bitcast(I32),
             )
 
-        later = late_pool.tile([P, 3 * 4 * M + MT * S], F32, name="later", offset=0)
+        later = late_pool.tile([P, 3 * 4 * M + MT * S], F32, name="later", offset=0, align_bytes=256)
         for i in range(3):
             w_raw.append(later[:, 4 * M * i : 4 * M * (i + 1)].rearrange("p (j n) -> p j n", j=4))
         res = [later[:, 12 * M + t * S : 12 * M + (t + 1) * S] for t in range(MT)]

@@ -22,6 +22,7 @@ PAIRS = 2
 NT = S // N
 MT = M // P
 H = M // 2
+WARM_UPS = 4
 
 
 def tile_list_tab4_res_kernel(tc, tab, w, r, offs, out):
@@ -124,9 +125,7 @@ def tile_list_tab4_res_kernel(tc, tab, w, r, offs, out):
         def finish(bank, n, t):
             cols = slice(n * N, (n + 1) * N)
             nc.vector.tensor_tensor(out=res[t][:, cols], in0=bank[:], in1=res[t][:, cols], op=ADD)
-            if t == MT - 1:
-                nc.sync.dma_start(out=out[t * P : (t + 1) * P, cols], in_=res[t][:, cols])
-            elif n == NT - 1:
+            if n == NT - 1:
                 nc.sync.dma_start(out=out[t * P : (t + 1) * P, :], in_=res[t])
 
         tiles = [(n, t) for t in range(MT) for n in range(NT)]
@@ -148,24 +147,40 @@ def tile_list_tab4_res_kernel(tc, tab, w, r, offs, out):
         for first in (0, H):
             round_w(nc.scalar.copy, 0, first, first + H, keep, f"b0{first}")
             quantize_w(0, first, first + H)
+        for i in range(WARM_UPS):
+            nc.tensor.matmul_mx(
+                out=banks[early[-1]][:],
+                lhsT=w_codes[0][:, 0:P].bitcast(E4M3X4),
+                lhsT_scale=w_scales[0][:, 0:P],
+                rhs=codes[(0, 0)][:, 0 : 2 * N].bitcast(E2M1X4),
+                rhs_scale=picked_rows[:, 0:N],
+                start=True,
+                stop=True,
+            )
         early_pass(0)
-        for n in range(NT):
-            gather(1, n, keep, f"p1{n}")
+        gather(1, 0, keep, "p10")
+        gather(1, 1, keep, "p11")
         part(1, 0, keep, "c10")
-        for first, last, tag in ((0, P, "turn1"), (P, H, "turn2"), (H, M, "b1")):
+        for first, last, tag in ((0, P, "turn1"), (P, H, "turn2"), (H, H + P, "b12")):
             round_w(nc.scalar.copy, 1, first, last, keep, tag)
             quantize_w(1, first, last)
         early_pass(1)
         part(1, 1, keep, "turn1")
-        part(1, 2, keep, "turn2")
-        for first, last in ((0, P), (P, H), (H, M)):
-            round_w(nc.scalar.copy, 2, first, last, keep, f"b2{first}")
+        gather(1, 2, keep, "turn2")
+        for first, last, tag in ((0, P, "turn3"), (P, H, "b21"), (H, H + P, "b22")):
+            round_w(nc.scalar.copy, 2, first, last, keep, tag)
             quantize_w(2, first, last)
+        part(1, 2, keep, "turn3")
         early_pass(2)
-        round_w(nc.vector.tensor_copy, 3, 0, H, keep, "b30")
-        round_w(nc.scalar.copy, 3, H, M, keep, "b31")
-        quantize_w(3, 0, H)
-        quantize_w(3, H, M)
+        round_w(nc.vector.tensor_copy, 3, 0, P, keep, "b30")
+        round_w(nc.scalar.copy, 3, P, H, keep, "b31")
+        round_w(nc.scalar.copy, 3, H, H + P, keep, "b32")
+        quantize_w(3, 0, P)
+        quantize_w(3, P, H)
+        quantize_w(3, H, H + P)
+        for a in range(1, PASSES):
+            round_w(nc.scalar.copy, a, H + P, M, keep, f"b{a}3")
+            quantize_w(a, H + P, M)
         early_pass(3)
         for n, t in late:
             bank = psum.tile([P, N], F32, name="bank")

@@ -22,7 +22,6 @@ PAIRS = 2
 NT = S // N
 MT = M // P
 H = M // 2
-WARM_UPS = 4
 
 
 def tile_list_tab4_res_kernel(tc, tab, w, r, offs, out):
@@ -33,10 +32,10 @@ def tile_list_tab4_res_kernel(tc, tab, w, r, offs, out):
         psum = ctx.enter_context(tc.psum_pool(name="psum", bufs=8))
 
         offsets = keep.tile([P, S // 16], U16, name="offsets")
-        scale_rows = late_pool.tile([P, T], U8, name="scale_rows", offset=0, align_bytes=256)
+        scale_rows = late_pool.tile([P, T], U8, name="scale_rows", offset=4 * T - T // 2, align_bytes=256)
         picked_rows = keep.tile([P, S], U8, name="picked_rows", align_bytes=256)
         planes = keep.tile([P, PASSES * S], U8, name="planes", align_bytes=256)
-        table = [keep.tile([P, T], I32, name=f"table{m}", align_bytes=256)[:] for m in range(PAIRS)]
+        table = [keep.tile([P, T], I32, name="table0", align_bytes=256)[:]]
         w_raw = [keep.tile([P, 4, M], F32, name="w_raw0", align_bytes=256)[:]]
         w_codes = [keep.tile([P, M], U32, name=f"w_codes{a}", align_bytes=64) for a in range(PASSES)]
         w_scales = [keep.tile([P, M], U8, name=f"w_scales{a}", align_bytes=64) for a in range(PASSES)]
@@ -49,11 +48,10 @@ def tile_list_tab4_res_kernel(tc, tab, w, r, offs, out):
         nc.vector.memset(planes[:].bitcast(I32), 0)
 
         nc.sync.dma_start(out=offsets[:], in_=offs)
-        for m in range(PAIRS):
-            nc.sync.dma_start(
-                out=scale_rows[32 + m : 96 : 2, :].bitcast(I32),
-                in_=tab[m : m + 1, 512 * T : 544 * T].rearrange("o (h q t) -> (o q) h t", h=2, t=T).bitcast(I32),
-            )
+        nc.sync.dma_start(
+            out=scale_rows[32:96, :].bitcast(I32),
+            in_=tab[:, 512 * T : 544 * T].rearrange("m (q t) -> q m t", t=T).bitcast(I32),
+        )
 
         def load_table(m):
             words = tab[m : m + 1, 0 : 512 * T].rearrange("o (p x) -> (o p) x", p=P)
@@ -64,16 +62,23 @@ def tile_list_tab4_res_kernel(tc, tab, w, r, offs, out):
 
         load_table(0)
         load_w(0)
-        load_table(1)
 
         nc.vector.tensor_copy(picked_rows[:], scale_rows[:].indirect(offsets[:]))
-        for q in (0, 2, 1, 3):
-            nc.sync.dma_start(
-                out=planes[32 * q : 32 * q + 4, :].bitcast(I32).rearrange("p (c s) -> p c s", c=PASSES),
-                in_=picked_rows[32 + 16 * q : 48 + 16 * q, :].bitcast(I32),
-            )
 
-        later = late_pool.tile([P, 3 * 4 * M + MT * S], F32, name="later", offset=0, align_bytes=256)
+        def move_rows(h):
+            for q in (0, 2, 1, 3):
+                first = 32 + 32 * h + 8 * q
+                nc.sync.dma_start(
+                    out=planes[32 * q : 32 * q + 4, 2 * h * S : 2 * (h + 1) * S].bitcast(I32).rearrange("p (c s) -> p c s", c=2),
+                    in_=picked_rows[first : first + 8, :].bitcast(I32),
+                )
+
+        move_rows(0)
+        table.append(late_pool.tile([P, T], I32, name="table1", offset=0, align_bytes=256)[:])
+        load_table(1)
+        move_rows(1)
+
+        later = late_pool.tile([P, 3 * 4 * M + MT * S], F32, name="later", offset=4 * T, align_bytes=256)
         for i in range(3):
             w_raw.append(later[:, 4 * M * i : 4 * M * (i + 1)].rearrange("p (j n) -> p j n", j=4))
         res = [later[:, 12 * M + t * S : 12 * M + (t + 1) * S] for t in range(MT)]
@@ -147,16 +152,6 @@ def tile_list_tab4_res_kernel(tc, tab, w, r, offs, out):
         for first in (0, H):
             round_w(nc.scalar.copy, 0, first, first + H, keep, f"b0{first}")
             quantize_w(0, first, first + H)
-        for i in range(WARM_UPS):
-            nc.tensor.matmul_mx(
-                out=banks[early[-1]][:],
-                lhsT=w_codes[0][:, 0:P].bitcast(E4M3X4),
-                lhsT_scale=w_scales[0][:, 0:P],
-                rhs=codes[(0, 0)][:, 0 : 2 * N].bitcast(E2M1X4),
-                rhs_scale=picked_rows[:, 0:N],
-                start=True,
-                stop=True,
-            )
         early_pass(0)
         gather(1, 0, keep, "p10")
         gather(1, 1, keep, "p11")

@@ -33,12 +33,12 @@ def tile_list_tab4_res_kernel(tc, tab, w, r, offs, out):
 
         offsets = keep.tile([P, S // 16], U16, name="offsets")
         scale_rows = late_pool.tile([P, T], U8, name="scale_rows", offset=4 * T - T // 2, align_bytes=256)
-        picked_rows = keep.tile([P, S], U8, name="picked_rows", align_bytes=256)
+        picked_rows = late_pool.tile([P, S], U8, name="picked_rows", offset=16 * T, align_bytes=256)
         planes = keep.tile([P, PASSES * S], U8, name="planes", align_bytes=256)
         table = [keep.tile([P, T], I32, name="table0", align_bytes=256)[:]]
         w_raw = [keep.tile([P, 4, M], F32, name="w_raw0", align_bytes=256)[:]]
-        w_codes = [keep.tile([P, M], U32, name=f"w_codes{a}", align_bytes=64) for a in range(PASSES)]
-        w_scales = [keep.tile([P, M], U8, name=f"w_scales{a}", align_bytes=64) for a in range(PASSES)]
+        w_codes = {}
+        w_scales = {}
         picked = {}
         codes = {}
         w_bf = {}
@@ -108,19 +108,29 @@ def tile_list_tab4_res_kernel(tc, tab, w, r, offs, out):
             )
 
         def quantize_w(a, first, last):
+            width = last - first
+            if (a, first) == (0, H):
+                words = late_pool.tile([P, width], U32, name="held_codes", offset=16 * T, align_bytes=256)
+                plane = late_pool.tile([P, width], U8, name="held_scales", offset=16 * T + 4 * width, align_bytes=256)
+            else:
+                words = keep.tile([P, width], U32, name=f"w_codes{a}_{first}", align_bytes=64)
+                plane = keep.tile([P, width], U8, name=f"w_scales{a}_{first}", align_bytes=64)
             nc.vector.quantize_mx(
-                out=w_codes[a][:, first:last].bitcast(E4M3X4),
-                scales=w_scales[a][:, first:last],
+                out=words[:].bitcast(E4M3X4),
+                scales=plane[:],
                 in_=w_bf[(a, first)][:].rearrange("p n j -> p (n j)"),
             )
+            for t in range(first // P, last // P):
+                w_codes[(a, t)] = words[:, t * P - first : (t + 1) * P - first]
+                w_scales[(a, t)] = plane[:, t * P - first : (t + 1) * P - first]
 
         def multiply(bank, a, n, t):
             m, h = divmod(a, 2)
             plane = (2 * h + m) * S + n * N
             nc.tensor.matmul_mx(
                 out=bank[:],
-                lhsT=w_codes[a][:, t * P : (t + 1) * P].bitcast(E4M3X4),
-                lhsT_scale=w_scales[a][:, t * P : (t + 1) * P],
+                lhsT=w_codes[(a, t)].bitcast(E4M3X4),
+                lhsT_scale=w_scales[(a, t)],
                 rhs=codes[(m, n)][:, 2 * N * h : 2 * N * (h + 1)].bitcast(E2M1X4),
                 rhs_scale=planes[:, plane : plane + N],
                 start=(a == 0),
@@ -149,13 +159,13 @@ def tile_list_tab4_res_kernel(tc, tab, w, r, offs, out):
         gather(0, 2, keep, "p02")
         part(0, 1, keep, "c01")
         part(0, 2, keep, "c02")
-        for first in (0, H):
-            round_w(nc.scalar.copy, 0, first, first + H, keep, f"b0{first}")
-            quantize_w(0, first, first + H)
+        for first, last in ((0, H), (H + P, M), (H, H + P)):
+            round_w(nc.scalar.copy, 0, first, last, keep, "turn0" if first == H else f"b0{first}")
+            quantize_w(0, first, last)
         early_pass(0)
         gather(1, 0, keep, "p10")
         gather(1, 1, keep, "p11")
-        part(1, 0, keep, "c10")
+        part(1, 0, keep, "turn0")
         for first, last, tag in ((0, P, "turn1"), (P, H, "turn2"), (H, H + P, "b12")):
             round_w(nc.scalar.copy, 1, first, last, keep, tag)
             quantize_w(1, first, last)

@@ -88,20 +88,21 @@ def tile_list_tab4_res_kernel(tc, tab, w, r, offs, out):
             nc.sync.dma_start(out=res[t], in_=r[t * P : (t + 1) * P, :])
 
         def gather(m, n, pool, tag):
-            picked[(m, n)] = pool.tile([P, N], U32, name="picked%d%d" % (m, n), tag=tag, align_bytes=64)
+            picked[(m, n)] = pool.tile([P, N], U32, name="picked%d%d" % (m, n), tag=tag, align_bytes=256)
             nc.vector.tensor_copy(
                 picked[(m, n)][:],
                 table[m].bitcast(U32).indirect(offsets[:, n * N // 16 : (n + 1) * N // 16]),
             )
 
         def part(m, n, pool, tag):
-            codes[(m, n)] = pool.tile([P, 4 * N], U8, name="codes%d%d" % (m, n), tag=tag, align_bytes=64)
-            dst = codes[(m, n)][:].bitcast(U16).rearrange("p (h t) -> p h t", h=2)
+            padded = pool.tile([P, 64 + 4 * N], U8, name="codes%d%d" % (m, n), tag=tag, align_bytes=256)
+            codes[(m, n)] = padded[:, 64:]
+            dst = codes[(m, n)].bitcast(U16).rearrange("p (h t) -> p h t", h=2)
             src = picked[(m, n)][:].bitcast(U16).rearrange("p (t h) -> p h t", h=2)
             nc.vector.tensor_copy(dst, src)
 
         def round_w(copy, a, first, last, pool, tag):
-            w_bf[(a, first)] = pool.tile([P, last - first, 4], BF16, name="w_bf%d_%d" % (a, first), tag=tag, align_bytes=64)
+            w_bf[(a, first)] = pool.tile([P, last - first, 4], BF16, name="w_bf%d_%d" % (a, first), tag=tag, align_bytes=256)
             copy(
                 w_bf[(a, first)][:].rearrange("p (c i) j -> p c j i", i=4),
                 w_raw[a][:, :, first:last].rearrange("p j (c i) -> p c j i", i=4),
@@ -110,37 +111,37 @@ def tile_list_tab4_res_kernel(tc, tab, w, r, offs, out):
         def quantize_w(a, first, last):
             width = last - first
             if (a, first) == (0, H):
-                words = late_pool.tile([P, width], U32, name="held_codes", offset=16 * T, align_bytes=256)
-                plane = late_pool.tile([P, width], U8, name="held_scales", offset=16 * T + 4 * width, align_bytes=256)
+                words = late_pool.tile([P, 32 + width], U32, name="held_codes", offset=16 * T, align_bytes=256)[:, 32:]
+                plane = late_pool.tile([P, 192 + width], U8, name="held_scales", offset=16 * T + 768, align_bytes=256)[:, 192:]
             else:
-                words = keep.tile([P, width], U32, name=f"w_codes{a}_{first}", align_bytes=64)
-                plane = keep.tile([P, width], U8, name=f"w_scales{a}_{first}", align_bytes=64)
+                words = keep.tile([P, 32 + width], U32, name=f"w_codes{a}_{first}", align_bytes=256)[:, 32:]
+                plane = keep.tile([P, 192 + width], U8, name=f"w_scales{a}_{first}", align_bytes=256)[:, 192:]
             nc.vector.quantize_mx(
-                out=words[:].bitcast(E4M3X4),
-                scales=plane[:],
+                out=words.bitcast(E4M3X4),
+                scales=plane,
                 in_=w_bf[(a, first)][:].rearrange("p n j -> p (n j)"),
             )
             for t in range(first // P, last // P):
                 w_codes[(a, t)] = words[:, t * P - first : (t + 1) * P - first]
                 w_scales[(a, t)] = plane[:, t * P - first : (t + 1) * P - first]
 
-        def multiply(bank, a, n, t):
+        def multiply(bank, a, n, t, first=0, last=N):
             m, h = divmod(a, 2)
             plane = (2 * h + m) * S + n * N
             nc.tensor.matmul_mx(
-                out=bank[:],
+                out=bank[:, 0 : last - first],
                 lhsT=w_codes[(a, t)].bitcast(E4M3X4),
                 lhsT_scale=w_scales[(a, t)],
-                rhs=codes[(m, n)][:, 2 * N * h : 2 * N * (h + 1)].bitcast(E2M1X4),
-                rhs_scale=planes[:, plane : plane + N],
+                rhs=codes[(m, n)][:, 2 * (N * h + first) : 2 * (N * h + last)].bitcast(E2M1X4),
+                rhs_scale=planes[:, plane + first : plane + last],
                 start=(a == 0),
                 stop=(a == PASSES - 1),
             )
 
-        def finish(bank, n, t):
-            cols = slice(n * N, (n + 1) * N)
-            nc.vector.tensor_tensor(out=res[t][:, cols], in0=bank[:], in1=res[t][:, cols], op=ADD)
-            if n == NT - 1:
+        def finish(bank, n, t, first=0, last=N):
+            cols = slice(n * N + first, n * N + last)
+            nc.vector.tensor_tensor(out=res[t][:, cols], in0=bank[:, 0 : last - first], in1=res[t][:, cols], op=ADD)
+            if n == NT - 1 and last == N:
                 nc.sync.dma_start(out=out[t * P : (t + 1) * P, :], in_=res[t])
 
         tiles = [(n, t) for t in range(MT) for n in range(NT)]
@@ -187,8 +188,9 @@ def tile_list_tab4_res_kernel(tc, tab, w, r, offs, out):
             round_w(nc.scalar.copy, a, H + P, M, keep, f"b{a}3")
             quantize_w(a, H + P, M)
         early_pass(3)
-        for n, t in late:
+        pieces = [(n, t, 0, N) for n, t in late[:-1]] + [late[-1] + (first, first + N // 2) for first in (0, N // 2)]
+        for n, t, first, last in pieces:
             bank = psum.tile([P, N], F32, name="bank")
             for a in range(PASSES):
-                multiply(bank, a, n, t)
-            finish(bank, n, t)
+                multiply(bank, a, n, t, first, last)
+            finish(bank, n, t, first, last)

@@ -142,7 +142,8 @@ def tile_list_tab4_res_kernel(tc, tab, w, r, offs, out):
             cols = slice(n * N + first, n * N + last)
             nc.vector.tensor_tensor(out=res[t][:, cols], in0=bank[:, 0 : last - first], in1=res[t][:, cols], op=ADD)
             if n == NT - 1 and last == N:
-                nc.sync.dma_start(out=out[t * P : (t + 1) * P, :], in_=res[t])
+                queue = nc.scalar if t % 2 else nc.sync
+                queue.dma_start(out=out[t * P : (t + 1) * P, :], in_=res[t])
 
         tiles = [(n, t) for t in range(MT) for n in range(NT)]
         early, late = tiles[:8], tiles[8:]

from contextlib import ExitStack

import concourse.mybir as mybir

K, M, T, S = 2048, 512, 4096, 1536
FLOPS = 2 * K * M * S

F32 = mybir.dt.float32
BF16 = mybir.dt.bfloat16
I32 = mybir.dt.int32
U32 = mybir.dt.uint32
U16 = mybir.dt.uint16
U8 = mybir.dt.uint8
E4M3X4 = mybir.dt.float8_e4m3fn_x4
E2M1X4 = mybir.dt.float4_e2m1fn_x4
ADD = mybir.AluOpType.add

P = 128
N = 512
PASSES = 4
PAIRS = 2
NT = S // N
MT = M // P
H = M // 2


def tile_list_tab4_res_kernel(tc, tab, w, r, offs, out):
    nc = tc.nc
    with ExitStack() as ctx:
        keep = ctx.enter_context(tc.tile_pool(name="keep", bufs=1))
        late_pool = ctx.enter_context(tc.tile_pool(name="late_pool", bufs=1))
        psum = ctx.enter_context(tc.psum_pool(name="psum", bufs=8))

        offsets = keep.tile([P, S // 16], U16, name="offsets")
        scale_rows = late_pool.tile([P, T], U8, name="scale_rows", offset=4 * T - T // 2, align_bytes=256)
        picked_rows = late_pool.tile([P, S], U8, name="picked_rows", offset=16 * T, align_bytes=256)
        planes = keep.tile([P, PASSES * S], U8, name="planes", align_bytes=256)
        table = [keep.tile([P, T], I32, name="table0", align_bytes=256)[:]]
        w_raw = [keep.tile([P, 4, M], F32, name="w_raw0", align_bytes=256)[:]]
        w_codes = {}
        w_scales = {}
        picked = {}
        codes = {}
        w_bf = {}

        nc.gpsimd.memset(scale_rows[0:32, :].bitcast(I32), 0)
        nc.gpsimd.memset(scale_rows[96:128, :].bitcast(I32), 0)
        nc.vector.memset(planes[:].bitcast(I32), 0)

        nc.sync.dma_start(out=offsets[:], in_=offs)
        nc.sync.dma_start(
            out=scale_rows[32:96, :].bitcast(I32),
            in_=tab[:, 512 * T : 544 * T].rearrange("m (q t) -> q m t", t=T).bitcast(I32),
        )

        def load_table(m):
            words = tab[m : m + 1, 0 : 512 * T].rearrange("o (p x) -> (o p) x", p=P)
            nc.sync.dma_start(out=table[m], in_=words.bitcast(I32))

        def load_w(a):
            nc.sync.dma_start(out=w_raw[a], in_=w[512 * a : 512 * (a + 1), :].rearrange("(p j) n -> p j n", j=4))

        load_table(0)
        load_w(0)

        nc.vector.tensor_copy(picked_rows[:], scale_rows[:].indirect(offsets[:]))

        def move_rows(h):
            for q in (0, 2, 1, 3):
                first = 32 + 32 * h + 8 * q
                nc.sync.dma_start(
                    out=planes[32 * q : 32 * q + 4, 2 * h * S : 2 * (h + 1) * S].bitcast(I32).rearrange("p (c s) -> p c s", c=2),
                    in_=picked_rows[first : first + 8, :].bitcast(I32),
                )

        move_rows(0)
        table.append(late_pool.tile([P, T], I32, name="table1", offset=0, align_bytes=256)[:])
        load_table(1)
        move_rows(1)

        later = late_pool.tile([P, 3 * 4 * M + MT * S], F32, name="later", offset=4 * T, align_bytes=256)
        for i in range(3):
            w_raw.append(later[:, 4 * M * i : 4 * M * (i + 1)].rearrange("p (j n) -> p j n", j=4))
        res = [later[:, 12 * M + t * S : 12 * M + (t + 1) * S] for t in range(MT)]
        for a in range(1, PASSES):
            load_w(a)
        for t in range(MT):
            nc.sync.dma_start(out=res[t], in_=r[t * P : (t + 1) * P, :])

        def gather(m, n, pool, tag):
            picked[(m, n)] = pool.tile([P, N], U32, name="picked%d%d" % (m, n), tag=tag, align_bytes=256)
            nc.vector.tensor_copy(
                picked[(m, n)][:],
                table[m].bitcast(U32).indirect(offsets[:, n * N // 16 : (n + 1) * N // 16]),
            )

        def part(m, n, pool, tag):
            padded = pool.tile([P, 64 + 4 * N], U8, name="codes%d%d" % (m, n), tag=tag, align_bytes=256)
            codes[(m, n)] = padded[:, 64:]
            dst = codes[(m, n)].bitcast(U16).rearrange("p (h t) -> p h t", h=2)
            src = picked[(m, n)][:].bitcast(U16).rearrange("p (t h) -> p h t", h=2)
            nc.vector.tensor_copy(dst, src)

        def round_w(copy, a, first, last, pool, tag):
            w_bf[(a, first)] = pool.tile([P, last - first, 4], BF16, name="w_bf%d_%d" % (a, first), tag=tag, align_bytes=256)
            copy(
                w_bf[(a, first)][:].rearrange("p (c i) j -> p c j i", i=4),
                w_raw[a][:, :, first:last].rearrange("p j (c i) -> p c j i", i=4),
            )

        def quantize_w(a, first, last):
            width = last - first
            if (a, first) == (0, H):
                words = late_pool.tile([P, 32 + width], U32, name="held_codes", offset=16 * T, align_bytes=256)[:, 32:]
                plane = late_pool.tile([P, 192 + width], U8, name="held_scales", offset=16 * T + 768, align_bytes=256)[:, 192:]
            else:
                words = keep.tile([P, 32 + width], U32, name=f"w_codes{a}_{first}", align_bytes=256)[:, 32:]
                plane = keep.tile([P, 192 + width], U8, name=f"w_scales{a}_{first}", align_bytes=256)[:, 192:]
            nc.vector.quantize_mx(
                out=words.bitcast(E4M3X4),
                scales=plane,
                in_=w_bf[(a, first)][:].rearrange("p n j -> p (n j)"),
            )
            for t in range(first // P, last // P):
                w_codes[(a, t)] = words[:, t * P - first : (t + 1) * P - first]
                w_scales[(a, t)] = plane[:, t * P - first : (t + 1) * P - first]

        def multiply(bank, a, n, t, first=0, last=N):
            m, h = divmod(a, 2)
            plane = (2 * h + m) * S + n * N
            nc.tensor.matmul_mx(
                out=bank[:, 0 : last - first],
                lhsT=w_codes[(a, t)].bitcast(E4M3X4),
                lhsT_scale=w_scales[(a, t)],
                rhs=codes[(m, n)][:, 2 * (N * h + first) : 2 * (N * h + last)].bitcast(E2M1X4),
                rhs_scale=planes[:, plane + first : plane + last],
                start=(a == 0),
                stop=(a == PASSES - 1),
            )

        def finish(bank, n, t, first=0, last=N):
            cols = slice(n * N + first, n * N + last)
            nc.vector.tensor_tensor(out=res[t][:, cols], in0=bank[:, 0 : last - first], in1=res[t][:, cols], op=ADD)
            if n == NT - 1 and last == N:
                queue = nc.scalar if t % 2 else nc.sync
                queue.dma_start(out=out[t * P : (t + 1) * P, :], in_=res[t])

        tiles = [(n, t) for t in range(MT) for n in range(NT)]
        early, late = tiles[:8], tiles[8:]
        banks = {nt: psum.tile([P, N], F32, name="bank") for nt in early}

        def early_pass(a):
            for n, t in early:
                multiply(banks[(n, t)], a, n, t)
                if a == PASSES - 1:
                    finish(banks[(n, t)], n, t)

        gather(0, 0, keep, "p00")
        gather(0, 1, keep, "p01")
        part(0, 0, keep, "c00")
        gather(0, 2, keep, "p02")
        part(0, 1, keep, "c01")
        part(0, 2, keep, "c02")
        for first, last in ((0, H), (H + P, M), (H, H + P)):
            round_w(nc.scalar.copy, 0, first, last, keep, "turn0" if first == H else f"b0{first}")
            quantize_w(0, first, last)
        early_pass(0)
        gather(1, 0, keep, "p10")
        gather(1, 1, keep, "p11")
        part(1, 0, keep, "turn0")
        for first, last, tag in ((0, P, "turn1"), (P, H, "turn2"), (H, H + P, "b12")):
            round_w(nc.scalar.copy, 1, first, last, keep, tag)
            quantize_w(1, first, last)
        early_pass(1)
        part(1, 1, keep, "turn1")
        gather(1, 2, keep, "turn2")
        for first, last, tag in ((0, P, "turn3"), (P, H, "b21"), (H, H + P, "b22")):
            round_w(nc.scalar.copy, 2, first, last, keep, tag)
            quantize_w(2, first, last)
        part(1, 2, keep, "turn3")
        early_pass(2)
        round_w(nc.vector.tensor_copy, 3, 0, P, keep, "b30")
        round_w(nc.scalar.copy, 3, P, H, keep, "b31")
        round_w(nc.scalar.copy, 3, H, H + P, keep, "b32")
        quantize_w(3, 0, P)
        quantize_w(3, P, H)
        quantize_w(3, H, H + P)
        for a in range(1, PASSES):
            round_w(nc.scalar.copy, a, H + P, M, keep, f"b{a}3")
            quantize_w(a, H + P, M)
        early_pass(3)
        pieces = [(n, t, 0, N) for n, t in late[:-1]] + [late[-1] + (first, first + N // 2) for first in (0, N // 2)]
        for n, t, first, last in pieces:
            bank = psum.tile([P, N], F32, name="bank")
            for a in range(PASSES):
                multiply(bank, a, n, t, first, last)
            finish(bank, n, t, first, last)
